import numpy as np
import ml_dtypes


def mxq(x, axis, fmt="e4m3"):
    dtype, down = {"e4m3": (ml_dtypes.float8_e4m3fn, 7), "e5m2": (ml_dtypes.float8_e5m2, 14)}[fmt]
    v = np.moveaxis(np.asarray(x, np.float32).astype(ml_dtypes.bfloat16).astype(np.float64), axis, -1)
    blocks = v.reshape(v.shape[:-1] + (-1, 32))
    amax = np.abs(blocks).max(-1, keepdims=True)
    byte = np.maximum(np.where(amax > 0, np.frexp(amax)[1] - 1 + 127, 0) - down, 1)
    scale = np.exp2(byte - 127.0)
    codes = (blocks / scale).astype(np.float32).astype(dtype).astype(np.float64)
    return np.moveaxis((codes * scale).reshape(v.shape), -1, axis)


WIDE = False


def mx_kscale(k):
    if not WIDE:
        return np.ones(k)
    levels = np.array([10, -10, 5, -5, 0])
    if k % 512:
        return np.exp2(np.random.permutation(np.resize(levels, k // 32))).repeat(32)
    a = np.empty((k // 512, 16))
    for p in range(k // 512):
        a[p, :8] = np.random.permutation(np.resize(levels, 8))
        for g in range(8):
            far = levels[np.abs(levels - a[p, g]) >= 10]
            a[p, g + 8] = far[np.random.randint(len(far))]
    return np.exp2(a.ravel()).repeat(32)


def f64(x):
    return np.asarray(x).astype(np.float64)


E2M1 = np.array([0.0, 0.5, 1.0, 1.5, 2.0, 3.0, 4.0, 6.0, -0.0, -0.5, -1.0, -1.5, -2.0, -3.0, -4.0, -6.0])


def pack_weight(w, fmt):
    k, n = w.shape
    w = f64(np.asarray(w, np.float32).astype(ml_dtypes.bfloat16)).reshape(k // 32, 32, n)
    amax = np.abs(w).max(1)
    if fmt == "e4m3":
        byte = np.frexp(amax)[1] - 1 + 127 - 7
    else:
        mant, ex = np.frexp(amax / 6.0)
        byte = np.where(mant > 0.5, ex, ex - 1) + 127
    byte = np.clip(np.where(amax > 0, byte, 1), 1, 254)
    scaled = (w * np.exp2(127.0 - byte)[:, None, :]).reshape(k, n).astype(np.float32)
    by_word = np.ascontiguousarray(scaled.reshape(k // 512, 128, 4, n).transpose(0, 1, 3, 2))
    if fmt == "e4m3":
        words = by_word.astype(ml_dtypes.float8_e4m3fn).view(np.uint8)
    else:
        c = by_word.astype(ml_dtypes.float4_e2m1fn).view(np.uint8) & 0xF
        words = (c[..., 0::2] | (c[..., 1::2] << 4)).reshape(k // 512, 128, 2 * n)
    return np.ascontiguousarray(words), np.ascontiguousarray(byte.astype(np.uint8).reshape(k // 512, 16, n))


def unpack_weight(words, scales, fmt):
    g, _, n = scales.shape
    words = np.ascontiguousarray(words).reshape(g, 128, n, -1)
    if fmt == "e4m3":
        vals = words.view(ml_dtypes.float8_e4m3fn).astype(np.float64)
    else:
        nib = np.empty((g, 128, n, 4), np.uint8)
        nib[..., 0::2] = words & 0xF
        nib[..., 1::2] = words >> 4
        vals = E2M1[nib]
    vals = vals * np.repeat(np.exp2(scales.astype(np.float64) - 127.0), 8, axis=1)[..., None]
    return vals.transpose(0, 1, 3, 2).reshape(g * 512, n)


K, L, T, N = 1024, 1024, 512, 512


def setup_inputs():
    n = np.random.standard_normal
    fk = mx_kscale(K)
    fl = mx_kscale(L)
    wap = pack_weight(n((K, N)) * 1 / np.sqrt(K) * fk[:, None], "e2m1")
    xqp = pack_weight(n((L, T)) / fl[:, None], "e4m3")
    wqp = pack_weight(n((L, N)) * 1 / np.sqrt(L) * fl[:, None], "e2m1")
    return {
        "xf": (n((K, T)) / fk[:, None]).astype(np.float32),
        "ta": (np.random.uniform(0.5, 2.0, (K, 1))).astype(np.float32),
        "tb": (np.random.uniform(-1.0, 1.0, (K, 1))).astype(np.float32),
        "td": (np.random.uniform(-0.7, 0.7, (K, 1))).astype(np.float32),
        "wa_words": wap[0],
        "wa_scales": wap[1],
        "xq_words": xqp[0],
        "xq_scales": xqp[1],
        "wq_words": wqp[0],
        "wq_scales": wqp[1],
    }


def reference(xf, ta, tb, td, wa_words, wa_scales, xq_words, xq_scales, wq_words, wq_scales):
    wau = unpack_weight(wa_words, wa_scales, "e2m1")
    xqu = unpack_weight(xq_words, xq_scales, "e4m3")
    wqu = unpack_weight(wq_words, wq_scales, "e2m1")
    x1 = np.pad(f64(xf), ((0, 0), (1, 0)))[:, :T]
    x2 = np.pad(f64(xf), ((0, 0), (2, 0)))[:, :T]
    u = f64(ta) * f64(xf) + f64(tb) * x1 + f64(td) * x2
    uq = mxq(u, 0, "e4m3")
    z = wau.T @ uq + wqu.T @ xqu
    y = np.maximum(z, 0.0)
    return y

@@ -1,0 +1,275 @@
+from contextlib import ExitStack
+
+import concourse.mybir as mybir
+
+K, L, T, N = 1024, 1024, 512, 512
+FLOPS = 2 * (K + L) * T * N
+
+F32 = mybir.dt.float32
+BF16 = mybir.dt.bfloat16
+I32 = mybir.dt.int32
+U32 = mybir.dt.uint32
+U8 = mybir.dt.uint8
+E4M3 = mybir.dt.float8_e4m3fn_x4
+E2M1 = mybir.dt.float4_e2m1fn_x4
+ALU = mybir.AluOpType
+ACT = mybir.ActivationFunctionType
+
+P = 128
+PACK = 4
+PASSES = 2
+ROWS = PASSES * PACK
+CHUNK = 128
+CHUNKS = T // CHUNK
+NTILES = N // P
+PAD = 8
+HALF = T // 2
+RUN = 4
+
+
+def tile_mix_tapped_and_given_kernel(
+    tc, xf, ta, tb, td, wa_words, wa_scales, xq_words, xq_scales, wq_words, wq_scales, out
+):
+    nc = tc.nc
+    with ExitStack() as ctx:
+        sb = ctx.enter_context(tc.tile_pool(name="sb", bufs=1))
+        ps = ctx.enter_context(tc.psum_pool(name="ps", bufs=1))
+        ctx.enter_context(tc.manual_schedule())
+
+        xs = sb.tile([P, ROWS, PAD + T], F32, name="xs")
+        zeros = sb.tile([P, ROWS, PAD], F32, name="zeros")
+        tap_a = sb.tile([P, PASSES, PACK], F32, name="tap_a")
+        tap_b = sb.tile([P, PASSES, PACK], F32, name="tap_b")
+        tap_d = sb.tile([P, PASSES, PACK], F32, name="tap_d")
+        now = sb.tile([P, ROWS, T], F32, name="now")
+        two = [sb.tile([P, PACK, T], F32, name="two%d" % g) for g in range(PASSES)]
+        old = [sb.tile([P, PACK, T], F32, name="old%d" % g) for g in range(PASSES)]
+        rows_bf = sb.tile([P, PACK, HALF], BF16, name="rows_bf")
+        grouped = {}
+        codes = {}
+        scales = {}
+        for g in range(PASSES):
+            for c in range(CHUNKS):
+                grouped[g, c] = sb.tile([P, CHUNK * PACK], BF16, name="grouped%d%d" % (g, c), align_bytes=64)
+                codes[g, c] = sb.tile([P, CHUNK], U32, name="codes%d%d" % (g, c), align_bytes=64)
+                scales[g, c] = sb.tile([P, CHUNK], U8, name="scales%d%d" % (g, c), align_bytes=64)
+        wa_sb = sb.tile([P, PASSES, 2 * N], U8, name="wa_sb", align_bytes=64)
+        wq_sb = sb.tile([P, PASSES, 2 * N], U8, name="wq_sb", align_bytes=64)
+        xq_sb = [sb.tile([P, PACK * T], U8, name="xq_sb%d" % z, align_bytes=64) for z in range(PASSES)]
+        wa_sc = sb.tile([P, PASSES, N], U8, name="wa_sc", align_bytes=64)
+        wq_sc = sb.tile([P, PASSES, N], U8, name="wq_sc", align_bytes=64)
+        xq_sc = sb.tile([P, PASSES, T], U8, name="xq_sc", align_bytes=64)
+
+        x_rows = xf.rearrange("(g p j) t -> p g j t", g=PASSES, j=PACK)
+        out_rows = out.rearrange("(nt p) t -> p nt t", p=P)
+        order = [2, 3, 0, 1]
+        last = order[-1]
+
+        banks = {}
+        for c in range(CHUNKS):
+            if c == last:
+                for h in range(2):
+                    banks[c, h] = ps.tile([P, 2 * CHUNK], F32, name="bank%d%d" % (c, h))
+            else:
+                banks[c, 0] = ps.tile([P, NTILES * CHUNK], F32, name="bank%d" % c)
+        result = {key: sb.tile([P, banks[key].shape[1]], F32, name="result%d%d" % key) for key in banks}
+
+        def tap(tile, r):
+            return tile[:, r // PACK, r % PACK : r % PACK + 1]
+
+        def x_at(r, delay, lo, hi):
+            return xs[:, r, PAD - delay + lo : PAD - delay + hi]
+
+        def load_x(r):
+            nc.sync.dma_start(out=xs[:, r, PAD:], in_=x_rows[:, r // PACK, r % PACK, :])
+
+        def load_tap(tile, src):
+            nc.scalar.dma_start(out=tile[:], in_=src.rearrange("(g p j) o -> p g (j o)", g=PASSES, j=PACK))
+
+        def load_words(tile, src):
+            nc.sync.dma_start(out=tile[:].bitcast(I32), in_=src.bitcast(I32).rearrange("z p c -> p z c"))
+
+        def load_xq(z):
+            nc.sync.dma_start(
+                out=xq_sb[z][:].bitcast(I32), in_=xq_words[z].rearrange("p c r -> p (c r)").bitcast(I32)
+            )
+
+        def load_scales(eng, tile, src):
+            for q in range(4):
+                eng.dma_start(
+                    out=tile[32 * q : 32 * q + 4, :, :].bitcast(I32),
+                    in_=src.bitcast(I32)[:, 4 * q : 4 * q + 4, :].rearrange("z r c -> r z c"),
+                )
+
+        def now_scalar(r):
+            nc.scalar.activation(out=now[:, r, :], in_=x_at(r, 0, 0, T), func=ACT.Copy, scale=tap(tap_a, r))
+
+        def now_vector(r, lo, hi):
+            nc.vector.tensor_scalar_mul(out=now[:, r, lo:hi], in0=x_at(r, 0, lo, hi), scalar1=tap(tap_a, r))
+
+        def old_scalar(r, lo, hi):
+            nc.scalar.activation(
+                out=old[r // PACK][:, r % PACK, lo:hi], in_=x_at(r, 2, lo, hi), func=ACT.Copy, scale=tap(tap_d, r)
+            )
+
+        def old_vector(r, lo, hi):
+            nc.vector.tensor_scalar_mul(
+                out=old[r // PACK][:, r % PACK, lo:hi], in0=x_at(r, 2, lo, hi), scalar1=tap(tap_d, r)
+            )
+
+        def add_second(r, lo, hi):
+            nc.vector.scalar_tensor_tensor(
+                out=two[r // PACK][:, r % PACK, lo:hi], in0=x_at(r, 1, lo, hi), scalar=tap(tap_b, r),
+                in1=now[:, r, lo:hi], op0=ALU.mult, op1=ALU.add,
+            )
+
+        def add_third(r):
+            nc.vector.scalar_tensor_tensor(
+                out=rows_bf[:, r, :], in0=x_at(r, 2, 0, HALF), scalar=tap(tap_d, r),
+                in1=two[0][:, r, 0:HALF], op0=ALU.mult, op1=ALU.add,
+            )
+
+        def walk(rows, c):
+            return rows[:, :, c * CHUNK : (c + 1) * CHUNK].rearrange("p j (b i) -> p b j i", i=RUN)
+
+        def walk_grouped(g, c):
+            return grouped[g, c][:].rearrange("p (b i j) -> p b j i", i=RUN, j=PACK)
+
+        def group_copy(c):
+            nc.scalar.copy(out=walk_grouped(0, c), in_=walk(rows_bf, c))
+
+        def group_add(g, c):
+            nc.vector.tensor_tensor(out=walk_grouped(g, c), in0=walk(two[g], c), in1=walk(old[g], c), op=ALU.add)
+
+        def quantize(g, c):
+            nc.vector.quantize_mx(out=codes[g, c][:].bitcast(E4M3), scales=scales[g, c][:], in_=grouped[g, c][:])
+
+        def bank_cols(c, nt):
+            if c == last:
+                return banks[c, nt // 2][:, (nt % 2) * CHUNK : (nt % 2 + 1) * CHUNK], nt % 2 == 0, nt % 2 == 1
+            return banks[c, 0][:, nt * CHUNK : (nt + 1) * CHUNK], nt == 0, nt == NTILES - 1
+
+        def passes(c, w_sb, w_sc, z, rhs, rhs_scale, opens, closes):
+            for nt in range(NTILES):
+                dst, first, final = bank_cols(c, nt)
+                nc.tensor.matmul_mx(
+                    out=dst,
+                    lhsT=w_sb[:, z, 2 * P * nt : 2 * P * (nt + 1)].bitcast(E2M1),
+                    lhsT_scale=w_sc[:, z, P * nt : P * (nt + 1)],
+                    rhs=rhs,
+                    rhs_scale=rhs_scale,
+                    start=opens and first,
+                    stop=closes and final,
+                )
+
+        def given_passes(z, c):
+            passes(
+                c, wq_sb, wq_sc, z,
+                xq_sb[z][:, PACK * CHUNK * c : PACK * CHUNK * (c + 1)].bitcast(E4M3),
+                xq_sc[:, z, CHUNK * c : CHUNK * (c + 1)], z == 0, False,
+            )
+
+        def tapped_passes(g, c):
+            passes(c, wa_sb, wa_sc, g, codes[g, c][:].bitcast(E4M3), scales[g, c][:], False, g == PASSES - 1)
+
+        def finish(c):
+            cols = slice(c * CHUNK, (c + 1) * CHUNK)
+            if c == last:
+                nc.scalar.activation(out=result[c, 0][:], in_=banks[c, 0][:], func=ACT.Relu)
+                nc.scalar.dma_start(
+                    out=out_rows[:, 0:2, cols], in_=result[c, 0][:].rearrange("p (nt t) -> p nt t", t=CHUNK)
+                )
+                nc.vector.tensor_scalar_max(out=result[c, 1][:], in0=banks[c, 1][:], scalar1=0.0)
+                nc.sync.dma_start(
+                    out=out_rows[:, 2:4, cols], in_=result[c, 1][:].rearrange("p (nt t) -> p nt t", t=CHUNK)
+                )
+            else:
+                nc.scalar.activation(out=result[c, 0][:], in_=banks[c, 0][:], func=ACT.Relu)
+                nc.sync.dma_start(
+                    out=out_rows[:, :, cols], in_=result[c, 0][:].rearrange("p (nt t) -> p nt t", t=CHUNK)
+                )
+
+        load_x(0)
+        load_tap(tap_a, ta)
+        load_tap(tap_b, tb)
+        load_tap(tap_d, td)
+        nc.vector.memset(zeros[:], 0.0)
+        nc.scalar.activation(out=xs[:, :, 0:PAD], in_=zeros[:], func=ACT.Relu)
+        nc.gpsimd.memset(wq_sc[:].bitcast(I32), 0)
+        nc.vector.memset(xq_sc[:].bitcast(I32), 0)
+        nc.vector.memset(wa_sc[:].bitcast(I32), 0)
+        load_scales(nc.gpsimd, wq_sc, wq_scales)
+        for r in (1, 2, 3):
+            load_x(r)
+        load_words(wq_sb, wq_words)
+        load_xq(0)
+        load_scales(nc.sync, xq_sc, xq_scales)
+        load_x(4)
+        load_x(5)
+        load_xq(1)
+        load_x(6)
+        load_x(7)
+        load_words(wa_sb, wa_words)
+        load_scales(nc.sync, wa_sc, wa_scales)
+
+        for z in range(PASSES):
+            for c in order:
+                given_passes(z, c)
+
+        now_vector(0, 0, HALF)
+        now_vector(0, HALF, T)
+        old_scalar(0, HALF, T)
+        add_second(0, 0, HALF)
+        add_second(0, HALF, T)
+        add_third(0)
+        for r in (1, 2, 3):
+            now_scalar(r)
+        for r in (1, 2, 3):
+            old_scalar(r, HALF, T)
+        add_second(1, 0, T)
+        add_second(2, 0, T)
+        add_third(1)
+        add_second(3, 0, T)
+        add_third(2)
+        group_add(0, 2)
+        add_third(3)
+        group_add(0, 3)
+
+        now_scalar(4)
+        old_scalar(4, 0, T)
+        now_scalar(5)
+        now_scalar(6)
+        now_scalar(7)
+        old_scalar(5, 0, T)
+        old_scalar(6, 0, T)
+        group_copy(0)
+        group_copy(1)
+        quantize(0, 2)
+        add_second(4, 0, T)
+        quantize(0, 3)
+        for r in (5, 6):
+            add_second(r, 0, T)
+        old_vector(7, 0, T)
+        add_second(7, 0, T)
+        tapped_passes(0, 2)
+        tapped_passes(0, 3)
+        group_add(1, 2)
+        group_add(1, 3)
+        quantize(1, 2)
+        tapped_passes(1, 2)
+        finish(2)
+        quantize(0, 0)
+        tapped_passes(0, 0)
+        group_add(1, 0)
+        quantize(1, 3)
+        tapped_passes(1, 3)
+        finish(3)
+        quantize(0, 1)
+        tapped_passes(0, 1)
+        group_add(1, 1)
+        quantize(1, 0)
+        tapped_passes(1, 0)
+        finish(0)
+        quantize(1, 1)
+        tapped_passes(1, 1)
+        finish(1)

@@ -37,13 +37,12 @@ def tile_mix_tapped_and_given_kernel(
         ctx.enter_context(tc.manual_schedule())
 
         xs = sb.tile([P, ROWS, PAD + T], F32, name="xs")
-        zeros = sb.tile([P, ROWS, PAD], F32, name="zeros")
-        tap_a = sb.tile([P, PASSES, PACK], F32, name="tap_a")
-        tap_b = sb.tile([P, PASSES, PACK], F32, name="tap_b")
-        tap_d = sb.tile([P, PASSES, PACK], F32, name="tap_d")
+        tap_a = sb.tile([P, PASSES, 2 * PACK], F32, name="tap_a")
+        tap_b = sb.tile([P, PASSES, 2 * PACK], F32, name="tap_b")
+        tap_d = sb.tile([P, PASSES, 2 * PACK], F32, name="tap_d")
         now = sb.tile([P, ROWS, T], F32, name="now")
         two = [sb.tile([P, PACK, T], F32, name="two%d" % g) for g in range(PASSES)]
-        old = [sb.tile([P, PACK, T], F32, name="old%d" % g) for g in range(PASSES)]
+        old = {key: sb.tile([P, PACK, HALF], F32, name="old%d%d" % key) for key in ((0, 1), (1, 0), (1, 1))}
         rows_bf = sb.tile([P, PACK, HALF], BF16, name="rows_bf")
         grouped = {}
         codes = {}
@@ -53,8 +52,9 @@ def tile_mix_tapped_and_given_kernel(
                 grouped[g, c] = sb.tile([P, CHUNK * PACK], BF16, name="grouped%d%d" % (g, c), align_bytes=64)
                 codes[g, c] = sb.tile([P, CHUNK], U32, name="codes%d%d" % (g, c), align_bytes=64)
                 scales[g, c] = sb.tile([P, CHUNK], U8, name="scales%d%d" % (g, c), align_bytes=64)
-        wa_sb = sb.tile([P, PASSES, 2 * N], U8, name="wa_sb", align_bytes=64)
-        wq_sb = sb.tile([P, PASSES, 2 * N], U8, name="wq_sb", align_bytes=64)
+        wa_both = sb.tile([P, PASSES, 2 * N], U8, name="wa_both", align_bytes=64)
+        wa_sb = [wa_both[:, z, :] for z in range(PASSES)]
+        wq_sb = [sb.tile([P, 2 * N], U8, name="wq_sb%d" % z, align_bytes=64) for z in range(PASSES)]
         xq_sb = [sb.tile([P, PACK * T], U8, name="xq_sb%d" % z, align_bytes=64) for z in range(PASSES)]
         wa_sc = sb.tile([P, PASSES, N], U8, name="wa_sc", align_bytes=64)
         wq_sc = sb.tile([P, PASSES, N], U8, name="wq_sc", align_bytes=64)
@@ -62,7 +62,7 @@ def tile_mix_tapped_and_given_kernel(
 
         x_rows = xf.rearrange("(g p j) t -> p g j t", g=PASSES, j=PACK)
         out_rows = out.rearrange("(nt p) t -> p nt t", p=P)
-        order = [2, 3, 0, 1]
+        order = [0, 1, 2, 3]
         last = order[-1]
 
         banks = {}
@@ -80,14 +80,20 @@ def tile_mix_tapped_and_given_kernel(
         def x_at(r, delay, lo, hi):
             return xs[:, r, PAD - delay + lo : PAD - delay + hi]
 
-        def load_x(r):
-            nc.sync.dma_start(out=xs[:, r, PAD:], in_=x_rows[:, r // PACK, r % PACK, :])
+        def load_x(r, n, lo, hi):
+            j = r % PACK
+            nc.sync.dma_start(
+                out=xs[:, r : r + n, PAD + lo : PAD + hi], in_=x_rows[:, r // PACK, j : j + n, lo:hi]
+            )
 
         def load_tap(tile, src):
-            nc.scalar.dma_start(out=tile[:], in_=src.rearrange("(g p j) o -> p g (j o)", g=PASSES, j=PACK))
+            nc.scalar.dma_start(out=tile[:, :, 0:PACK], in_=src.rearrange("(g p j) o -> p g (j o)", g=PASSES, j=PACK))
 
         def load_words(tile, src):
             nc.sync.dma_start(out=tile[:].bitcast(I32), in_=src.bitcast(I32).rearrange("z p c -> p z c"))
+
+        def load_wq(z):
+            nc.sync.dma_start(out=wq_sb[z][:].bitcast(I32), in_=wq_words[z].bitcast(I32))
 
         def load_xq(z):
             nc.sync.dma_start(
@@ -95,26 +101,19 @@ def tile_mix_tapped_and_given_kernel(
             )
 
         def load_scales(eng, tile, src):
-            for q in range(4):
-                eng.dma_start(
-                    out=tile[32 * q : 32 * q + 4, :, :].bitcast(I32),
-                    in_=src.bitcast(I32)[:, 4 * q : 4 * q + 4, :].rearrange("z r c -> r z c"),
-                )
+            rows = src.bitcast(I32).rearrange("z (q r) c -> r q z c", r=4)
+            for r in range(4):
+                eng.dma_start(out=tile[r:P:32, :, :].bitcast(I32), in_=rows[r])
 
-        def now_scalar(r):
-            nc.scalar.activation(out=now[:, r, :], in_=x_at(r, 0, 0, T), func=ACT.Copy, scale=tap(tap_a, r))
+        def now_scalar(r, lo, hi):
+            nc.scalar.activation(out=now[:, r, lo:hi], in_=x_at(r, 0, lo, hi), func=ACT.Copy, scale=tap(tap_a, r))
 
         def now_vector(r, lo, hi):
             nc.vector.tensor_scalar_mul(out=now[:, r, lo:hi], in0=x_at(r, 0, lo, hi), scalar1=tap(tap_a, r))
 
         def old_scalar(r, lo, hi):
             nc.scalar.activation(
-                out=old[r // PACK][:, r % PACK, lo:hi], in_=x_at(r, 2, lo, hi), func=ACT.Copy, scale=tap(tap_d, r)
-            )
-
-        def old_vector(r, lo, hi):
-            nc.vector.tensor_scalar_mul(
-                out=old[r // PACK][:, r % PACK, lo:hi], in0=x_at(r, 2, lo, hi), scalar1=tap(tap_d, r)
+                out=old[r // PACK, lo // HALF][:, r % PACK, :], in_=x_at(r, 2, lo, hi), func=ACT.Copy, scale=tap(tap_d, r)
             )
 
         def add_second(r, lo, hi):
@@ -129,17 +128,22 @@ def tile_mix_tapped_and_given_kernel(
                 in1=two[0][:, r, 0:HALF], op0=ALU.mult, op1=ALU.add,
             )
 
-        def walk(rows, c):
-            return rows[:, :, c * CHUNK : (c + 1) * CHUNK].rearrange("p j (b i) -> p b j i", i=RUN)
+        def walk(rows, lo, hi):
+            return rows[:, :, lo:hi].rearrange("p j (b i) -> p b j i", i=RUN)
 
-        def walk_grouped(g, c):
-            return grouped[g, c][:].rearrange("p (b i j) -> p b j i", i=RUN, j=PACK)
+        def walk_grouped(g, c, lo, hi):
+            return grouped[g, c][:, PACK * lo : PACK * hi].rearrange("p (b i j) -> p b j i", i=RUN, j=PACK)
 
         def group_copy(c):
-            nc.scalar.copy(out=walk_grouped(0, c), in_=walk(rows_bf, c))
+            nc.scalar.copy(out=walk_grouped(0, c, 0, CHUNK), in_=walk(rows_bf, c * CHUNK, (c + 1) * CHUNK))
 
-        def group_add(g, c):
-            nc.vector.tensor_tensor(out=walk_grouped(g, c), in0=walk(two[g], c), in1=walk(old[g], c), op=ALU.add)
+        def group_add(g, c, lo=0, hi=CHUNK):
+            nc.vector.tensor_tensor(
+                out=walk_grouped(g, c, lo, hi),
+                in0=walk(two[g], c * CHUNK + lo, c * CHUNK + hi),
+                in1=walk(old[g, c // 2], c % 2 * CHUNK + lo, c % 2 * CHUNK + hi),
+                op=ALU.add,
+            )
 
         def quantize(g, c):
             nc.vector.quantize_mx(out=codes[g, c][:].bitcast(E4M3), scales=scales[g, c][:], in_=grouped[g, c][:])
@@ -154,7 +158,7 @@ def tile_mix_tapped_and_given_kernel(
                 dst, first, final = bank_cols(c, nt)
                 nc.tensor.matmul_mx(
                     out=dst,
-                    lhsT=w_sb[:, z, 2 * P * nt : 2 * P * (nt + 1)].bitcast(E2M1),
+                    lhsT=w_sb[z][:, 2 * P * nt : 2 * P * (nt + 1)].bitcast(E2M1),
                     lhsT_scale=w_sc[:, z, P * nt : P * (nt + 1)],
                     rhs=rhs,
                     rhs_scale=rhs_scale,
@@ -189,87 +193,95 @@ def tile_mix_tapped_and_given_kernel(
                     out=out_rows[:, :, cols], in_=result[c, 0][:].rearrange("p (nt t) -> p nt t", t=CHUNK)
                 )
 
-        load_x(0)
+        LO = (0, HALF)
+        HI = (HALF, T)
+        load_x(0, 1, *LO)
         load_tap(tap_a, ta)
         load_tap(tap_b, tb)
         load_tap(tap_d, td)
-        nc.vector.memset(zeros[:], 0.0)
-        nc.scalar.activation(out=xs[:, :, 0:PAD], in_=zeros[:], func=ACT.Relu)
-        nc.gpsimd.memset(wq_sc[:].bitcast(I32), 0)
-        nc.vector.memset(xq_sc[:].bitcast(I32), 0)
+        nc.vector.memset(xs[:, 0:PACK, 0:PAD], 0.0)
+        nc.scalar.activation(out=xs[:, PACK:ROWS, 0:PAD], in_=xs[:, 0:PACK, 0:PAD], func=ACT.Relu)
+        nc.gpsimd.memset(xq_sc[:].bitcast(I32), 0)
+        nc.vector.memset(wq_sc[:].bitcast(I32), 0)
         nc.vector.memset(wa_sc[:].bitcast(I32), 0)
-        load_scales(nc.gpsimd, wq_sc, wq_scales)
+        load_scales(nc.gpsimd, xq_sc, xq_scales)
+        load_x(0, 1, *HI)
         for r in (1, 2, 3):
-            load_x(r)
-        load_words(wq_sb, wq_words)
+            load_x(r, 1, 0, T)
+        load_wq(0)
         load_xq(0)
-        load_scales(nc.sync, xq_sc, xq_scales)
-        load_x(4)
-        load_x(5)
+        load_scales(nc.sync, wq_sc, wq_scales)
+        load_x(4, 2, 0, T)
+        load_x(6, 2, *LO)
+        load_wq(1)
         load_xq(1)
-        load_x(6)
-        load_x(7)
-        load_words(wa_sb, wa_words)
+        load_x(6, 2, *HI)
+        load_words(wa_both, wa_words)
         load_scales(nc.sync, wa_sc, wa_scales)
 
         for z in range(PASSES):
             for c in order:
                 given_passes(z, c)
 
-        now_vector(0, 0, HALF)
-        now_vector(0, HALF, T)
-        old_scalar(0, HALF, T)
-        add_second(0, 0, HALF)
-        add_second(0, HALF, T)
+        now_vector(0, *LO)
+        now_vector(0, *HI)
+        old_scalar(0, *HI)
+        for r in (1, 2, 3):
+            now_scalar(r, *LO)
+            now_scalar(r, *HI)
+        for r in (1, 2, 3):
+            old_scalar(r, *HI)
+        add_second(0, *LO)
+        add_second(0, *HI)
         add_third(0)
-        for r in (1, 2, 3):
-            now_scalar(r)
-        for r in (1, 2, 3):
-            old_scalar(r, HALF, T)
-        add_second(1, 0, T)
-        add_second(2, 0, T)
+        add_second(1, *LO)
+        add_second(2, *LO)
         add_third(1)
-        add_second(3, 0, T)
+        add_second(3, *LO)
         add_third(2)
-        group_add(0, 2)
         add_third(3)
-        group_add(0, 3)
-
-        now_scalar(4)
-        old_scalar(4, 0, T)
-        now_scalar(5)
-        now_scalar(6)
-        now_scalar(7)
-        old_scalar(5, 0, T)
-        old_scalar(6, 0, T)
         group_copy(0)
         group_copy(1)
-        quantize(0, 2)
-        add_second(4, 0, T)
-        quantize(0, 3)
-        for r in (5, 6):
-            add_second(r, 0, T)
-        old_vector(7, 0, T)
-        add_second(7, 0, T)
-        tapped_passes(0, 2)
-        tapped_passes(0, 3)
-        group_add(1, 2)
-        group_add(1, 3)
-        quantize(1, 2)
-        tapped_passes(1, 2)
-        finish(2)
+        for r in (1, 2, 3):
+            add_second(r, *HI)
         quantize(0, 0)
-        tapped_passes(0, 0)
-        group_add(1, 0)
-        quantize(1, 3)
-        tapped_passes(1, 3)
-        finish(3)
+        group_add(0, 2)
+        group_add(0, 3)
         quantize(0, 1)
+        tapped_passes(0, 0)
         tapped_passes(0, 1)
+
+        now_scalar(4, 0, T)
+        now_scalar(5, 0, T)
+        for half in (LO, HI):
+            now_scalar(6, *half)
+            now_scalar(7, *half)
+            for r in (4, 5, 6, 7):
+                old_scalar(r, *half)
+        add_second(4, 0, T)
+        add_second(5, 0, T)
+        add_second(6, *LO)
+        add_second(7, *LO)
+        quantize(0, 2)
+        quantize(0, 3)
+        group_add(1, 0)
         group_add(1, 1)
         quantize(1, 0)
         tapped_passes(1, 0)
         finish(0)
+        tapped_passes(0, 2)
+        tapped_passes(0, 3)
+        add_second(6, *HI)
+        add_second(7, *HI)
         quantize(1, 1)
         tapped_passes(1, 1)
         finish(1)
+        group_add(1, 2)
+        group_add(1, 3, 0, CHUNK // 2)
+        quantize(1, 2)
+        tapped_passes(1, 2)
+        finish(2)
+        group_add(1, 3, CHUNK // 2, CHUNK)
+        quantize(1, 3)
+        tapped_passes(1, 3)
+        finish(3)

from contextlib import ExitStack

import concourse.mybir as mybir

K, L, T, N = 1024, 1024, 512, 512
FLOPS = 2 * (K + L) * T * N

F32 = mybir.dt.float32
BF16 = mybir.dt.bfloat16
I32 = mybir.dt.int32
U32 = mybir.dt.uint32
U8 = mybir.dt.uint8
E4M3 = mybir.dt.float8_e4m3fn_x4
E2M1 = mybir.dt.float4_e2m1fn_x4
ALU = mybir.AluOpType
ACT = mybir.ActivationFunctionType

P = 128
PACK = 4
PASSES = 2
ROWS = PASSES * PACK
CHUNK = 128
CHUNKS = T // CHUNK
NTILES = N // P
PAD = 8
HALF = T // 2
RUN = 4


def tile_mix_tapped_and_given_kernel(
    tc, xf, ta, tb, td, wa_words, wa_scales, xq_words, xq_scales, wq_words, wq_scales, out
):
    nc = tc.nc
    with ExitStack() as ctx:
        sb = ctx.enter_context(tc.tile_pool(name="sb", bufs=1))
        ps = ctx.enter_context(tc.psum_pool(name="ps", bufs=1))
        ctx.enter_context(tc.manual_schedule())

        xs = sb.tile([P, ROWS, PAD + T], F32, name="xs")
        tap_a = sb.tile([P, PASSES, 2 * PACK], F32, name="tap_a")
        tap_b = sb.tile([P, PASSES, 2 * PACK], F32, name="tap_b")
        tap_d = sb.tile([P, PASSES, 2 * PACK], F32, name="tap_d")
        now = sb.tile([P, ROWS, T], F32, name="now")
        two = [sb.tile([P, PACK, T], F32, name="two%d" % g) for g in range(PASSES)]
        old = {key: sb.tile([P, PACK, HALF], F32, name="old%d%d" % key) for key in ((0, 1), (1, 0), (1, 1))}
        rows_bf = sb.tile([P, PACK, HALF], BF16, name="rows_bf")
        grouped = {}
        codes = {}
        scales = {}
        for g in range(PASSES):
            for c in range(CHUNKS):
                grouped[g, c] = sb.tile([P, CHUNK * PACK], BF16, name="grouped%d%d" % (g, c), align_bytes=64)
                codes[g, c] = sb.tile([P, CHUNK], U32, name="codes%d%d" % (g, c), align_bytes=64)
                scales[g, c] = sb.tile([P, CHUNK], U8, name="scales%d%d" % (g, c), align_bytes=64)
        wa_both = sb.tile([P, PASSES, 2 * N], U8, name="wa_both", align_bytes=64)
        wa_sb = [wa_both[:, z, :] for z in range(PASSES)]
        wq_sb = [sb.tile([P, 2 * N], U8, name="wq_sb%d" % z, align_bytes=64) for z in range(PASSES)]
        xq_sb = [sb.tile([P, PACK * T], U8, name="xq_sb%d" % z, align_bytes=64) for z in range(PASSES)]
        wa_sc = sb.tile([P, PASSES, N], U8, name="wa_sc", align_bytes=64)
        wq_sc = sb.tile([P, PASSES, N], U8, name="wq_sc", align_bytes=64)
        xq_sc = sb.tile([P, PASSES, T], U8, name="xq_sc", align_bytes=64)

        x_rows = xf.rearrange("(g p j) t -> p g j t", g=PASSES, j=PACK)
        out_rows = out.rearrange("(nt p) t -> p nt t", p=P)
        order = [0, 1, 2, 3]
        last = order[-1]

        banks = {}
        for c in range(CHUNKS):
            if c == last:
                for h in range(2):
                    banks[c, h] = ps.tile([P, 2 * CHUNK], F32, name="bank%d%d" % (c, h))
            else:
                banks[c, 0] = ps.tile([P, NTILES * CHUNK], F32, name="bank%d" % c)
        result = {key: sb.tile([P, banks[key].shape[1]], F32, name="result%d%d" % key) for key in banks}

        def tap(tile, r):
            return tile[:, r // PACK, r % PACK : r % PACK + 1]

        def x_at(r, delay, lo, hi):
            return xs[:, r, PAD - delay + lo : PAD - delay + hi]

        def load_x(r, n, lo, hi):
            j = r % PACK
            nc.sync.dma_start(
                out=xs[:, r : r + n, PAD + lo : PAD + hi], in_=x_rows[:, r // PACK, j : j + n, lo:hi]
            )

        def load_tap(tile, src):
            nc.scalar.dma_start(out=tile[:, :, 0:PACK], in_=src.rearrange("(g p j) o -> p g (j o)", g=PASSES, j=PACK))

        def load_words(tile, src):
            nc.sync.dma_start(out=tile[:].bitcast(I32), in_=src.bitcast(I32).rearrange("z p c -> p z c"))

        def load_wq(z):
            nc.sync.dma_start(out=wq_sb[z][:].bitcast(I32), in_=wq_words[z].bitcast(I32))

        def load_xq(z):
            nc.sync.dma_start(
                out=xq_sb[z][:].bitcast(I32), in_=xq_words[z].rearrange("p c r -> p (c r)").bitcast(I32)
            )

        def load_scales(eng, tile, src):
            rows = src.bitcast(I32).rearrange("z (q r) c -> r q z c", r=4)
            for r in range(4):
                eng.dma_start(out=tile[r:P:32, :, :].bitcast(I32), in_=rows[r])

        def now_scalar(r, lo, hi):
            nc.scalar.activation(out=now[:, r, lo:hi], in_=x_at(r, 0, lo, hi), func=ACT.Copy, scale=tap(tap_a, r))

        def now_vector(r, lo, hi):
            nc.vector.tensor_scalar_mul(out=now[:, r, lo:hi], in0=x_at(r, 0, lo, hi), scalar1=tap(tap_a, r))

        def old_scalar(r, lo, hi):
            nc.scalar.activation(
                out=old[r // PACK, lo // HALF][:, r % PACK, :], in_=x_at(r, 2, lo, hi), func=ACT.Copy, scale=tap(tap_d, r)
            )

        def add_second(r, lo, hi):
            nc.vector.scalar_tensor_tensor(
                out=two[r // PACK][:, r % PACK, lo:hi], in0=x_at(r, 1, lo, hi), scalar=tap(tap_b, r),
                in1=now[:, r, lo:hi], op0=ALU.mult, op1=ALU.add,
            )

        def add_third(r):
            nc.vector.scalar_tensor_tensor(
                out=rows_bf[:, r, :], in0=x_at(r, 2, 0, HALF), scalar=tap(tap_d, r),
                in1=two[0][:, r, 0:HALF], op0=ALU.mult, op1=ALU.add,
            )

        def walk(rows, lo, hi):
            return rows[:, :, lo:hi].rearrange("p j (b i) -> p b j i", i=RUN)

        def walk_grouped(g, c, lo, hi):
            return grouped[g, c][:, PACK * lo : PACK * hi].rearrange("p (b i j) -> p b j i", i=RUN, j=PACK)

        def group_copy(c):
            nc.scalar.copy(out=walk_grouped(0, c, 0, CHUNK), in_=walk(rows_bf, c * CHUNK, (c + 1) * CHUNK))

        def group_add(g, c, lo=0, hi=CHUNK):
            nc.vector.tensor_tensor(
                out=walk_grouped(g, c, lo, hi),
                in0=walk(two[g], c * CHUNK + lo, c * CHUNK + hi),
                in1=walk(old[g, c // 2], c % 2 * CHUNK + lo, c % 2 * CHUNK + hi),
                op=ALU.add,
            )

        def quantize(g, c):
            nc.vector.quantize_mx(out=codes[g, c][:].bitcast(E4M3), scales=scales[g, c][:], in_=grouped[g, c][:])

        def bank_cols(c, nt):
            if c == last:
                return banks[c, nt // 2][:, (nt % 2) * CHUNK : (nt % 2 + 1) * CHUNK], nt % 2 == 0, nt % 2 == 1
            return banks[c, 0][:, nt * CHUNK : (nt + 1) * CHUNK], nt == 0, nt == NTILES - 1

        def passes(c, w_sb, w_sc, z, rhs, rhs_scale, opens, closes):
            for nt in range(NTILES):
                dst, first, final = bank_cols(c, nt)
                nc.tensor.matmul_mx(
                    out=dst,
                    lhsT=w_sb[z][:, 2 * P * nt : 2 * P * (nt + 1)].bitcast(E2M1),
                    lhsT_scale=w_sc[:, z, P * nt : P * (nt + 1)],
                    rhs=rhs,
                    rhs_scale=rhs_scale,
                    start=opens and first,
                    stop=closes and final,
                )

        def given_passes(z, c):
            passes(
                c, wq_sb, wq_sc, z,
                xq_sb[z][:, PACK * CHUNK * c : PACK * CHUNK * (c + 1)].bitcast(E4M3),
                xq_sc[:, z, CHUNK * c : CHUNK * (c + 1)], z == 0, False,
            )

        def tapped_passes(g, c):
            passes(c, wa_sb, wa_sc, g, codes[g, c][:].bitcast(E4M3), scales[g, c][:], False, g == PASSES - 1)

        def finish(c):
            cols = slice(c * CHUNK, (c + 1) * CHUNK)
            if c == last:
                nc.scalar.activation(out=result[c, 0][:], in_=banks[c, 0][:], func=ACT.Relu)
                nc.scalar.dma_start(
                    out=out_rows[:, 0:2, cols], in_=result[c, 0][:].rearrange("p (nt t) -> p nt t", t=CHUNK)
                )
                nc.vector.tensor_scalar_max(out=result[c, 1][:], in0=banks[c, 1][:], scalar1=0.0)
                nc.sync.dma_start(
                    out=out_rows[:, 2:4, cols], in_=result[c, 1][:].rearrange("p (nt t) -> p nt t", t=CHUNK)
                )
            else:
                nc.scalar.activation(out=result[c, 0][:], in_=banks[c, 0][:], func=ACT.Relu)
                nc.sync.dma_start(
                    out=out_rows[:, :, cols], in_=result[c, 0][:].rearrange("p (nt t) -> p nt t", t=CHUNK)
                )

        LO = (0, HALF)
        HI = (HALF, T)
        load_x(0, 1, *LO)
        load_tap(tap_a, ta)
        load_tap(tap_b, tb)
        load_tap(tap_d, td)
        nc.vector.memset(xs[:, 0:PACK, 0:PAD], 0.0)
        nc.scalar.activation(out=xs[:, PACK:ROWS, 0:PAD], in_=xs[:, 0:PACK, 0:PAD], func=ACT.Relu)
        nc.gpsimd.memset(xq_sc[:].bitcast(I32), 0)
        nc.vector.memset(wq_sc[:].bitcast(I32), 0)
        nc.vector.memset(wa_sc[:].bitcast(I32), 0)
        load_scales(nc.gpsimd, xq_sc, xq_scales)
        load_x(0, 1, *HI)
        for r in (1, 2, 3):
            load_x(r, 1, 0, T)
        load_wq(0)
        load_xq(0)
        load_scales(nc.sync, wq_sc, wq_scales)
        load_x(4, 2, 0, T)
        load_x(6, 2, *LO)
        load_wq(1)
        load_xq(1)
        load_x(6, 2, *HI)
        load_words(wa_both, wa_words)
        load_scales(nc.sync, wa_sc, wa_scales)

        for z in range(PASSES):
            for c in order:
                given_passes(z, c)

        now_vector(0, *LO)
        now_vector(0, *HI)
        old_scalar(0, *HI)
        for r in (1, 2, 3):
            now_scalar(r, *LO)
            now_scalar(r, *HI)
        for r in (1, 2, 3):
            old_scalar(r, *HI)
        add_second(0, *LO)
        add_second(0, *HI)
        add_third(0)
        add_second(1, *LO)
        add_second(2, *LO)
        add_third(1)
        add_second(3, *LO)
        add_third(2)
        add_third(3)
        group_copy(0)
        group_copy(1)
        for r in (1, 2, 3):
            add_second(r, *HI)
        quantize(0, 0)
        group_add(0, 2)
        group_add(0, 3)
        quantize(0, 1)
        tapped_passes(0, 0)
        tapped_passes(0, 1)

        now_scalar(4, 0, T)
        now_scalar(5, 0, T)
        for half in (LO, HI):
            now_scalar(6, *half)
            now_scalar(7, *half)
            for r in (4, 5, 6, 7):
                old_scalar(r, *half)
        add_second(4, 0, T)
        add_second(5, 0, T)
        add_second(6, *LO)
        add_second(7, *LO)
        quantize(0, 2)
        quantize(0, 3)
        group_add(1, 0)
        group_add(1, 1)
        quantize(1, 0)
        tapped_passes(1, 0)
        finish(0)
        tapped_passes(0, 2)
        tapped_passes(0, 3)
        add_second(6, *HI)
        add_second(7, *HI)
        quantize(1, 1)
        tapped_passes(1, 1)
        finish(1)
        group_add(1, 2)
        group_add(1, 3, 0, CHUNK // 2)
        quantize(1, 2)
        tapped_passes(1, 2)
        finish(2)
        group_add(1, 3, CHUNK // 2, CHUNK)
        quantize(1, 3)
        tapped_passes(1, 3)
        finish(3)
